import numpy as np, ml_dtypes
CORES = [40,41,42,43,44,45,46,47]
N = 8
import mx_ref
BF = ml_dtypes.bfloat16
def entries(a):
    return np.ascontiguousarray(a.T).reshape(-1)
def table(e):
    return np.ascontiguousarray(np.reshape(e, (-1, 16)).T).astype(np.int32)
def cols(t, e):
    v = np.concatenate([t.reshape(128, -1, 4), np.zeros((128, 1, 4), BF)], axis=1)
    return np.ascontiguousarray(v[:, e]).reshape(128, -1)
def decode(q):
    o = []
    for b in range(4):
        e = np.zeros((128, 128, 4), np.float32); e[np.arange(128), np.arange(128), b] = 1
        o.append(mx_ref.matmul(mx_ref.quantize(e.reshape(128, 512).astype(BF)), q))
    return np.stack(o, axis=2).reshape(128, -1)
def f(rng, *shape):
    return mx_ref.flush((rng.standard_normal(shape, dtype=np.float32) * np.exp2(rng.integers(-2, 3, shape[:-1] + (1,)))).astype(BF))
def wide(rng, *shape, cols=0):
    v = rng.standard_normal(shape, dtype=np.float32) * np.exp2(rng.integers(-12, 13, shape)).astype(np.float32)
    if cols: v *= np.repeat(np.exp2(rng.integers(-cols, cols + 1, shape[:-2] + (1, shape[-1] // 4))) * (rng.random(shape[:-2] + (1, shape[-1] // 4)) > 0.0625), 4, axis=-1).astype(np.float32)
    return mx_ref.flush(v.astype(BF))
TC, T, CAPP, O = 512, 256, 32, 2
def lists(rng, n, front=False):
    a = np.full((N, N, CAPP), -1)
    b = np.full((N, N, CAPP), -1)
    for s in range(N):
        for d in range(N):
            k = rng.permutation(CAPP)[:n[s, d]]
            a[s, d, k] = rng.integers(0, T, len(k)); b[d, s, k] = 0
    for d in range(N):
        used = b[d] == 0; u = int(used.sum())
        b[d][used] = np.arange(u) if front else rng.permutation(TC)[:u]
    return {"snd": np.stack([table(a[s]) for s in range(N)]), "plc": np.stack([table(b[d]) for d in range(N)])}
def tiles(rng):
    return {"kc": f(rng, N, 128, 4 * TC), "x": f(rng, N, 128, 4 * T), "qw": f(rng, N, 128, 512 * O)}
def setup_inputs(rng):
    return {**tiles(rng), **lists(rng, rng.integers(0, CAPP + 1, (N, N)))}
def setup_inputs_full(rng):
    return {**tiles(rng), **lists(rng, np.full((N, N), CAPP))}
def setup_inputs_few(rng):
    n = rng.integers(0, 3, (N, N))
    for d in range(N):
        o = rng.permutation([s for s in range(N) if s != d])
        n[o[0], d] = 0; n[o[1], d] = 1
    n[:, rng.integers(0, N)] = 0
    return {**tiles(rng), **lists(rng, n)}
def setup_inputs_front(rng):
    return {**tiles(rng), **lists(rng, rng.integers(1, CAPP + 1, (N, N)), front=True)}
def setup_inputs_own(rng):
    n = rng.integers(0, 3, (N, N)); n[np.arange(N), np.arange(N)] = CAPP
    return {**tiles(rng), **lists(rng, n)}
def setup_inputs_spread(rng):
    d = setup_inputs(rng); d["x"] = wide(rng, N, 128, 4 * T, cols=8); d["kc"] = wide(rng, N, 128, 4 * TC); return d
def check_inputs(d):
    b = []
    a = np.stack([entries(d["snd"][r]).reshape(N, CAPP) for r in range(N)])
    p = np.stack([entries(d["plc"][r]).reshape(N, CAPP) for r in range(N)])
    if a.min() < -1 or a.max() >= T: b.append("snd")
    if p.min() < -1 or p.max() >= TC: b.append("plc")
    if ((a.transpose(1, 0, 2) == -1) != (p == -1)).any(): b.append("plc is -1 exactly where the slot is empty")
    for r in range(N):
        v = p[r][p[r] != -1].tolist()
        if len(set(v)) != len(v): b.append("plc differs"); break
    return b
def reference(kc, x, qw, snd, plc):
    y = np.zeros((N, 128, O * TC), np.float32)
    for r in range(N):
        sent = np.concatenate([cols(x[s], entries(snd[s])[r * CAPP:(r + 1) * CAPP]) for s in range(N)], axis=1)
        got = decode(mx_ref.quantize(sent)).astype(BF).reshape(128, N * CAPP, 4)
        p = entries(plc[r]); used = p >= 0
        c = kc[r].reshape(128, TC, 4).copy()
        c[:, p[used]] = got[:, used]
        c = mx_ref.quantize(np.ascontiguousarray(c).reshape(128, 4 * TC))
        for o in range(O):
            y[r][:, TC * o:TC * o + TC] = mx_ref.matmul(mx_ref.quantize(np.ascontiguousarray(qw[r][:, 512 * o:512 * o + 512])), c)
    return {"y": y}

@@ -1,0 +1,274 @@
+from concourse.bass import DstId, RemoteDMATransfer
+from concourse.mybir import dt, AluOpType, ActivationFunctionType
+
+N = 8
+CAPP = 32
+XC = 256
+HC = 128
+TC = 512
+ARR = (N - 1) * CAPP
+PAD = 16
+VW = PAD + TC + 368
+
+SCRATCH = {
+    "xb": ("sbuf", [128, 4 * XC], "bfloat16"),
+    "kb": ("sbuf", [128, 4 * TC], "bfloat16"),
+    "qb": ("sbuf", [128, 4 * XC], "bfloat16"),
+    "ones": ("sbuf", [128, 516], "bfloat16"),
+    "ez": ("sbuf", [128, 516], "bfloat16"),
+    "eq": ("sbuf", [128, 512], "float8_e4m3fn_x4"),
+    "es": ("sbuf", [128, 512], "uint8"),
+    "xq": ("sbuf", [128, XC], "float8_e4m3fn_x4"),
+    "xs": ("sbuf", [128, XC], "uint8"),
+    "xd0": ("sbuf", [128, XC], "bfloat16"),
+    "xd1": ("sbuf", [128, XC], "bfloat16"),
+    "xd2": ("sbuf", [128, XC], "bfloat16"),
+    "xd3": ("sbuf", [128, XC], "bfloat16"),
+    "hb": ("sbuf", [128, 4 * XC], "bfloat16"),
+    "hq": ("sbuf", [128, XC], "float8_e4m3fn_x4"),
+    "hs": ("sbuf", [128, XC], "uint8"),
+    "aq": ("sbuf", [128, ARR], "float8_e4m3fn_x4"),
+    "asc": ("sbuf", [128, ARR], "uint8"),
+    "kq": ("sbuf", [128, TC], "float8_e4m3fn_x4"),
+    "ks": ("sbuf", [128, TC], "uint8"),
+    "wq": ("sbuf", [128, XC], "float8_e4m3fn_x4"),
+    "ws": ("sbuf", [128, XC], "uint8"),
+    "sl": ("sbuf", [128, 16], "int32"),
+    "so": ("sbuf", [128, 16], "uint16"),
+    "pl": ("sbuf", [128, 16], "int32"),
+    "pidx": ("sbuf", [128, 1], "int32"),
+    "pand": ("sbuf", [128, 1], "int32"),
+    "mlo": ("sbuf", [128, 1], "float32"),
+    "mhi": ("sbuf", [128, 1], "float32"),
+    "ktab": ("sbuf", [128, 16], "float32"),
+    "vals": ("sbuf", [128, XC], "float32"),
+    "vl": ("sbuf", [128, VW], "float32"),
+    "neg": ("sbuf", [128, 16], "float32"),
+    "p16": ("sbuf", [128, 16], "float32"),
+    "nk": ("sbuf", [128, 16], "float32"),
+    "pf": ("sbuf", [128, 16], "float32"),
+    "po": ("sbuf", [128, 16], "uint16"),
+    "t1": ("sbuf", [128, 512], "float32"),
+    "t2": ("sbuf", [128, 544], "float32"),
+    "u1": ("sbuf", [128, 32], "float32"),
+    "u2": ("sbuf", [128, 32], "float32"),
+    "inf32": ("sbuf", [128, 32], "float32"),
+    "inv": ("sbuf", [128, 32], "uint16"),
+    "w0": ("sbuf", [128, TC + XC], "float32"),
+    "w1": ("sbuf", [128, TC + XC], "float32"),
+    "y0": ("sbuf", [128, TC], "float32"),
+    "y1": ("sbuf", [128, TC], "float32"),
+    "pd0": ("psum", [128, 512], "float32"),
+    "pd1": ("psum", [128, 512], "float32"),
+    "pd2": ("psum", [128, 512], "float32"),
+    "pd3": ("psum", [128, 512], "float32"),
+    "pd4": ("psum", [128, 512], "float32"),
+    "pd5": ("psum", [128, 512], "float32"),
+    "py0": ("psum", [128, 512], "float32"),
+    "py1": ("psum", [128, 512], "float32"),
+}
+SEMAPHORES = (["lx0", "lx1", "lsnd", "lplc", "lqw", "lkc", "out", "arr", "sent",
+               "ones", "ez", "eq", "qx0", "qx1", "conv", "hq", "wq", "kq",
+               "pidx", "pand", "mask", "ktab", "vals", "vinit",
+               "ia", "ib", "ic", "id", "ie", "it", "ig", "ih", "inv",
+               "mo0", "mo1", "co0", "co1", "mk0", "mk1", "ck0", "ck1", "ma0", "ma1", "ca0", "ca1",
+               "y00", "y01", "y10", "y11"]
+              + ["m%d%d" % (h, b) for h in range(2) for b in range(4)]
+              + ["c%d%d" % (h, b) for h in range(2) for b in range(4)]
+              + ["g%d" % b for b in range(4)])
+
+
+def send_masks(core, dests, topo):
+    near = [d for d in dests if topo.die(d) == topo.die(core)]
+    far = [d for d in dests if topo.die(d) != topo.die(core)]
+    masks = {}
+    for group, first in ((far, 0), (near, 1)):
+        for k, d in enumerate(group):
+            e = topo.engines(core, d)
+            masks[d] = (1 << e[4 * k + first]) | (1 << e[4 * k + first + 2])
+    return masks
+
+
+def rank_program(g, core, T, topo):
+    rank = T.rank_of(core)
+    if rank is None:
+        return
+    S = T.sem
+    v, a, t, sy = g.vector, g.scalar, g.tensor, g.sync
+    COPY = ActivationFunctionType.Copy
+    A = AluOpType
+
+    for h in range(2):
+        sy.dma_start(T.xb[:, 512 * h:512 * h + 512], T.x[:, 512 * h:512 * h + 512]).then_inc(S["lx%d" % h], 16)
+    for k in range(8):
+        a.dma_start(T.sl[16 * k:16 * k + 16, :], T.snd[:, :]).then_inc(S.lsnd, 16)
+    for k in range(8):
+        sy.dma_start(T.pl[16 * k:16 * k + 16, :], T.plc[:, :]).then_inc(S.lplc, 16)
+    sy.dma_start(T.qb[:], T.qw[:, :]).then_inc(S.lqw, 16)
+    sy.dma_start(T.kb[:], T.kc[:, :]).then_inc(S.lkc, 16)
+
+    v.memset(T.ones[:], 1.0).then_inc(S.ones, 1)
+    g.wait_ge(S.ones, 1)
+    g.affine_select(T.ez[:], T.ones[:], [[-1, 516]], A.is_equal, 0.0, 3, 4).then_inc(S.ez, 1)
+    g.iota(T.pidx[:], [[1, 1]], 0, 1).then_inc(S.pidx, 1)
+    g.iota(T.ktab[:], [[16, 16]], PAD + TC, 1, allow_small_or_imprecise_dtypes=True).then_inc(S.ktab, 1)
+    cut = CAPP * (rank + 1)
+    nv = 1
+    g.iota(T.vals[:, 0:cut], [[1, cut]], TC + XC - cut, 0, allow_small_or_imprecise_dtypes=True).then_inc(S.vals, 1)
+    if cut < XC:
+        g.iota(T.vals[:, cut:XC], [[1, XC - cut]], TC, 0, allow_small_or_imprecise_dtypes=True).then_inc(S.vals, 1)
+        nv = 2
+    g.iota(T.vl[:, 0:544], [[1, 544]], -PAD, 0, allow_small_or_imprecise_dtypes=True).then_inc(S.vinit, 1)
+
+    v.wait_ge(S.ez, 1)
+    for b in range(4):
+        v.quantize_mx(T.eq[:, 128 * b:128 * b + 128], T.es[:, 128 * b:128 * b + 128],
+                      T.ez[:, 3 - b:3 - b + 512]).then_inc(S.eq, 1)
+    v.wait_ge(S.pidx, 1)
+    v.tensor_scalar(T.pand[:], T.pidx[:], 16, None, A.bitwise_and).then_inc(S.pand, 1)
+    v.wait_ge(S.pand, 1)
+    v.tensor_scalar(T.mlo[:], T.pand[:], 0.0, None, A.is_equal).then_inc(S.mask, 1)
+    v.tensor_scalar(T.mhi[:], T.pand[:], 0.0, None, A.is_gt).then_inc(S.mask, 1)
+
+    for h in range(2):
+        v.wait_ge(S["lx%d" % h], 16)
+        v.quantize_mx(T.xq[:, HC * h:HC * h + HC], T.xs[:, HC * h:HC * h + HC],
+                      T.xb[:, 512 * h:512 * h + 512]).then_inc(S["qx%d" % h], 1)
+    bank = {(0, 0): "pd0", (0, 1): "pd1", (0, 2): "pd2", (0, 3): "pd3",
+            (1, 0): "pd4", (1, 1): "pd5", (1, 2): "pd0", (1, 3): "pd1"}
+    t.wait_ge(S.eq, 4)
+    for h in range(2):
+        t.wait_ge(S["qx%d" % h], 1)
+        for b in range(4):
+            if (h, b) == (1, 2):
+                t.wait_ge(S.c00, 1)
+            if (h, b) == (1, 3):
+                t.wait_ge(S.c01, 1)
+            t.matmul_mx(T[bank[h, b]][:, 0:HC], T.eq[:, 128 * b:128 * b + 128], T.es[:, 128 * b:128 * b + 128],
+                        T.xq[:, HC * h:HC * h + HC], T.xs[:, HC * h:HC * h + HC], True, True).then_inc(S["m%d%d" % (h, b)], 1)
+    for h in range(2):
+        for b in (0, 2):
+            v.wait_ge(S["m%d%d" % (h, b)], 1)
+            v.tensor_copy(T["xd%d" % b][:, HC * h:HC * h + HC], T[bank[h, b]][:, 0:HC]).then_inc(S["c%d%d" % (h, b)], 1)
+        for b in (1, 3):
+            a.wait_ge(S["m%d%d" % (h, b)], 1)
+            a.activation(T["xd%d" % b][:, HC * h:HC * h + HC], T[bank[h, b]][:, 0:HC], COPY).then_inc(S["c%d%d" % (h, b)], 1)
+        if h == 0:
+            v.wait_ge(S.lsnd, 128)
+            v.tensor_copy(T.so[:], T.sl[:]).then_inc(S.conv, 1)
+
+    v.wait_ge(S.conv, 1)
+    for b in (0, 2):
+        v.wait_ge(S["c0%d" % b], 1)
+        v.wait_ge(S["c1%d" % b], 1)
+        v.tensor_copy(T.hb[:, b:4 * XC:4], T["xd%d" % b][:, 0:XC].indirect(T.so[:, 0:16])).then_inc(S["g%d" % b], 1)
+    a.wait_ge(S.conv, 1)
+    for b in (1, 3):
+        a.wait_ge(S["c0%d" % b], 1)
+        a.wait_ge(S["c1%d" % b], 1)
+        a.activation(T.hb[:, b:4 * XC:4], T["xd%d" % b][:, 0:XC].indirect(T.so[:, 0:16]), COPY).then_inc(S["g%d" % b], 1)
+    for b in range(4):
+        v.wait_ge(S["g%d" % b], 1)
+    v.quantize_mx(T.hq[:], T.hs[:], T.hb[:]).then_inc(S.hq, 1)
+
+    dests = [c for c in T.cores if c != core]
+    masks = send_masks(core, dests, topo)
+    g.wait_ge(S.hq, 1)
+    for planes in (False, True):
+        tr = []
+        for j in range(1, N):
+            d = (rank + j) % N
+            dst = T.cores[d]
+            k = (rank - d - 1) % N
+            rid, pid = topo.addr(dst)[:2]
+            if planes:
+                src, out = T.hs[:, CAPP * d:CAPP * d + CAPP], T.asc[:, CAPP * k:CAPP * k + CAPP]
+            else:
+                src = T.hq[:, CAPP * d:CAPP * d + CAPP].bitcast(dt.uint8)
+                out = T.aq[:, CAPP * k:CAPP * k + CAPP].bitcast(dt.uint8)
+            tr.append(RemoteDMATransfer(dst_ids=[DstId(rid=rid, pnc=pid)], dma_engine_mask=masks[dst],
+                                        remote_sem=S.arr, srcs=[src], dsts=[out]))
+        g.remote_dma_fused(tr, local_sem=S.sent)
+
+    v.wait_ge(S.lplc, 128)
+    v.tensor_scalar(T.neg[:], T.pl[:], 0.0, None, A.is_lt).then_inc(S.ia, 1)
+    v.tensor_scalar(T.p16[:], T.pl[:], float(PAD), None, A.add).then_inc(S.ia, 1)
+    v.wait_ge(S.lqw, 16)
+    v.quantize_mx(T.wq[:], T.ws[:], T.qb[:]).then_inc(S.wq, 1)
+    v.wait_ge(S.ia, 2)
+    v.wait_ge(S.ktab, 1)
+    v.tensor_tensor(T.nk[:], T.neg[:], T.ktab[:], A.mult).then_inc(S.ib, 1)
+    v.wait_ge(S.lkc, 16)
+    v.quantize_mx(T.kq[:], T.ks[:], T.kb[:]).then_inc(S.kq, 1)
+    v.wait_ge(S.ib, 1)
+    v.tensor_tensor(T.pf[:], T.nk[:], T.p16[:], A.max).then_inc(S.ic, 1)
+    v.wait_ge(S.ic, 1)
+    v.tensor_copy(T.po[:], T.pf[:]).then_inc(S.id, 1)
+    v.wait_ge(S.id, 1)
+    v.wait_ge(S.vals, nv)
+    v.wait_ge(S.vinit, 1)
+    v.tensor_copy(T.vl[:, 0:VW].indirect(T.po[:, 0:16]), T.vals[:, 0:XC]).then_inc(S.ie, 1)
+    v.wait_ge(S.ie, 1)
+    v.transpose(T.t1[:], T.vl[:, PAD:PAD + 512]).then_inc(S.it, 1)
+    v.transpose(T.t2[:], T.vl[:, 0:544]).then_inc(S.it, 1)
+    v.wait_ge(S.it, 2)
+    v.wait_ge(S.mask, 2)
+    v.tensor_scalar(T.u1[:, 0:32:2], T.t1[:, 0:512:32], T.mlo[:, 0:1], None, A.mult).then_inc(S.ig, 1)
+    v.tensor_scalar(T.u1[:, 1:32:2], T.t1[:, 0:512:32], T.mhi[:, 0:1], None, A.mult).then_inc(S.ig, 1)
+    v.tensor_scalar(T.u2[:, 0:32:2], T.t2[:, 0:512:32], T.mhi[:, 0:1], None, A.mult).then_inc(S.ig, 1)
+    v.tensor_scalar(T.u2[:, 1:32:2], T.t2[:, 32:544:32], T.mlo[:, 0:1], None, A.mult).then_inc(S.ig, 1)
+    v.wait_ge(S.ig, 4)
+    v.tensor_tensor(T.inf32[:], T.u1[:], T.u2[:], A.add).then_inc(S.ih, 1)
+    v.wait_ge(S.ih, 1)
+    v.tensor_copy(T.inv[:], T.inf32[:]).then_inc(S.inv, 1)
+
+    w = min(CAPP * rank, XC - 128)
+    own = CAPP * rank - w
+    t.wait_ge(S.wq, 1)
+    t.wait_ge(S.hq, 1)
+    for o in range(2):
+        t.matmul_mx(T["py%d" % o][:, 0:128], T.wq[:, 128 * o:128 * o + 128], T.ws[:, 128 * o:128 * o + 128],
+                    T.hq[:, w:w + 128], T.hs[:, w:w + 128], True, True).then_inc(S["mo%d" % o], 1)
+    for o in range(2):
+        a.wait_ge(S["mo%d" % o], 1)
+        a.activation(T["w%d" % o][:, TC + ARR:TC + XC], T["py%d" % o][:, own:own + CAPP], COPY).then_inc(S["co%d" % o], 1)
+    t.wait_ge(S.kq, 1)
+    for o in range(2):
+        t.wait_ge(S["co%d" % o], 1)
+        t.matmul_mx(T["py%d" % o][:, 0:TC], T.wq[:, 128 * o:128 * o + 128], T.ws[:, 128 * o:128 * o + 128],
+                    T.kq[:], T.ks[:], True, True).then_inc(S["mk%d" % o], 1)
+    for o in range(2):
+        a.wait_ge(S["mk%d" % o], 1)
+        a.activation(T["w%d" % o][:, 0:TC], T["py%d" % o][:, 0:TC], COPY).then_inc(S["ck%d" % o], 1)
+
+    for o in range(2):
+        t.wait_ge(S["ck%d" % o], 1)
+    t.wait_ge(S.arr, 2 * 2 * (N - 1))
+    for o in range(2):
+        t.matmul_mx(T["py%d" % o][:, 0:ARR], T.wq[:, 128 * o:128 * o + 128], T.ws[:, 128 * o:128 * o + 128],
+                    T.aq[:], T.asc[:], True, True).then_inc(S["ma%d" % o], 1)
+
+    v.wait_ge(S.ma0, 1)
+    v.tensor_copy(T.w0[:, TC:TC + ARR], T.py0[:, 0:ARR]).then_inc(S.ca0, 1)
+    v.wait_ge(S.ca0, 1)
+    v.wait_ge(S.co0, 1)
+    v.wait_ge(S.ck0, 1)
+    v.wait_ge(S.inv, 1)
+    a.wait_ge(S.ma1, 1)
+    a.activation(T.w1[:, TC:TC + ARR], T.py1[:, 0:ARR], COPY).then_inc(S.ca1, 1)
+    a.wait_ge(S.ca1, 1)
+    a.wait_ge(S.co1, 1)
+    a.wait_ge(S.ck1, 1)
+    a.wait_ge(S.inv, 1)
+    for h in range(2):
+        v.tensor_copy(T.y0[:, 256 * h:256 * h + 256],
+                      T.w0[:, 0:TC + XC].indirect(T.inv[:, 16 * h:16 * h + 16])).then_inc(S["y0%d" % h], 1)
+        a.activation(T.y1[:, 256 * h:256 * h + 256],
+                     T.w1[:, 0:TC + XC].indirect(T.inv[:, 16 * h:16 * h + 16]), COPY).then_inc(S["y1%d" % h], 1)
+    for h in range(2):
+        for o in range(2):
+            sy.wait_ge(S["y%d%d" % (o, h)], 1)
+            sy.dma_start(T.y[:, TC * o + 256 * h:TC * o + 256 * h + 256],
+                         T["y%d" % o][:, 256 * h:256 * h + 256]).then_inc(S.out, 16)
+    sy.wait_ge(S.out, 64)
+    g.wait_ge(S.sent, 2 * 2 * (N - 1))

@@ -1,81 +1,36 @@
 from concourse.bass import DstId, RemoteDMATransfer
 from concourse.mybir import dt, AluOpType, ActivationFunctionType
 
-N = 8
-CAPP = 32
-XC = 256
-HC = 128
-TC = 512
+N, CAPP, XC, HC, TC = 8, 32, 256, 128, 512
 ARR = (N - 1) * CAPP
-PAD = 16
-VW = PAD + TC + 368
+VI = TC + 32
+VW = VI + 368
+YP = ((0, 192), (192, 320))
+SECOND = ARR - HC
+CALLS = ((False, (0, 1, 2, 3)), (False, (4, 5, 6)), (True, (0, 1, 2, 3, 4, 5, 6)))
 
-SCRATCH = {
-    "xb": ("sbuf", [128, 4 * XC], "bfloat16"),
-    "kb": ("sbuf", [128, 4 * TC], "bfloat16"),
-    "qb": ("sbuf", [128, 4 * XC], "bfloat16"),
-    "ones": ("sbuf", [128, 516], "bfloat16"),
-    "ez": ("sbuf", [128, 516], "bfloat16"),
-    "eq": ("sbuf", [128, 512], "float8_e4m3fn_x4"),
-    "es": ("sbuf", [128, 512], "uint8"),
-    "xq": ("sbuf", [128, XC], "float8_e4m3fn_x4"),
-    "xs": ("sbuf", [128, XC], "uint8"),
-    "xd0": ("sbuf", [128, XC], "bfloat16"),
-    "xd1": ("sbuf", [128, XC], "bfloat16"),
-    "xd2": ("sbuf", [128, XC], "bfloat16"),
-    "xd3": ("sbuf", [128, XC], "bfloat16"),
-    "hb": ("sbuf", [128, 4 * XC], "bfloat16"),
-    "hq": ("sbuf", [128, XC], "float8_e4m3fn_x4"),
-    "hs": ("sbuf", [128, XC], "uint8"),
-    "aq": ("sbuf", [128, ARR], "float8_e4m3fn_x4"),
-    "asc": ("sbuf", [128, ARR], "uint8"),
-    "kq": ("sbuf", [128, TC], "float8_e4m3fn_x4"),
-    "ks": ("sbuf", [128, TC], "uint8"),
-    "wq": ("sbuf", [128, XC], "float8_e4m3fn_x4"),
-    "ws": ("sbuf", [128, XC], "uint8"),
-    "sl": ("sbuf", [128, 16], "int32"),
-    "so": ("sbuf", [128, 16], "uint16"),
-    "pl": ("sbuf", [128, 16], "int32"),
-    "pidx": ("sbuf", [128, 1], "int32"),
-    "pand": ("sbuf", [128, 1], "int32"),
-    "mlo": ("sbuf", [128, 1], "float32"),
-    "mhi": ("sbuf", [128, 1], "float32"),
-    "ktab": ("sbuf", [128, 16], "float32"),
-    "vals": ("sbuf", [128, XC], "float32"),
-    "vl": ("sbuf", [128, VW], "float32"),
-    "neg": ("sbuf", [128, 16], "float32"),
-    "p16": ("sbuf", [128, 16], "float32"),
-    "nk": ("sbuf", [128, 16], "float32"),
-    "pf": ("sbuf", [128, 16], "float32"),
-    "po": ("sbuf", [128, 16], "uint16"),
-    "t1": ("sbuf", [128, 512], "float32"),
-    "t2": ("sbuf", [128, 544], "float32"),
-    "u1": ("sbuf", [128, 32], "float32"),
-    "u2": ("sbuf", [128, 32], "float32"),
-    "inf32": ("sbuf", [128, 32], "float32"),
-    "inv": ("sbuf", [128, 32], "uint16"),
-    "w0": ("sbuf", [128, TC + XC], "float32"),
-    "w1": ("sbuf", [128, TC + XC], "float32"),
-    "y0": ("sbuf", [128, TC], "float32"),
-    "y1": ("sbuf", [128, TC], "float32"),
-    "pd0": ("psum", [128, 512], "float32"),
-    "pd1": ("psum", [128, 512], "float32"),
-    "pd2": ("psum", [128, 512], "float32"),
-    "pd3": ("psum", [128, 512], "float32"),
-    "pd4": ("psum", [128, 512], "float32"),
-    "pd5": ("psum", [128, 512], "float32"),
-    "py0": ("psum", [128, 512], "float32"),
-    "py1": ("psum", [128, 512], "float32"),
-}
-SEMAPHORES = (["lx0", "lx1", "lsnd", "lplc", "lqw", "lkc", "out", "arr", "sent",
-               "ones", "ez", "eq", "qx0", "qx1", "conv", "hq", "wq", "kq",
-               "pidx", "pand", "mask", "ktab", "vals", "vinit",
-               "ia", "ib", "ic", "id", "ie", "it", "ig", "ih", "inv",
-               "mo0", "mo1", "co0", "co1", "mk0", "mk1", "ck0", "ck1", "ma0", "ma1", "ca0", "ca1",
-               "y00", "y01", "y10", "y11"]
-              + ["m%d%d" % (h, b) for h in range(2) for b in range(4)]
-              + ["c%d%d" % (h, b) for h in range(2) for b in range(4)]
-              + ["g%d" % b for b in range(4)])
+
+def _buffers():
+    b = {}
+    for dtype, names in (("bfloat16", {"xb": 1024, "kb": 2048, "qb": 1024, "ones": 128, "idn": 128, "ez": 516, "xd0": XC, "xd1": XC, "xd2": XC, "xd3": XC, "hb": 1024}),
+                         ("int32", {"sl": 16, "pl": 16, "pidx": 1, "q15": 1, "q16": 1, "kneg": 16}),
+                         ("uint16", {"so": 16, "po": 16, "inv": 32, "eoff": 2}),
+                         ("float32", {"padc": 1, "padb": 1, "er": 1, "ef": 1, "vals": XC, "kio": VI, "vl": VW, "nk": 16, "pm": 16, "tr": VI,
+                                      "w0": TC + XC, "w1": TC + XC, "y0": TC, "y1": TC})):
+        for k, w in names.items():
+            b[k] = ("sbuf", [128, w], dtype)
+    for q, s, w in (("eq", "es", 512), ("xq", "xs", XC), ("hq0", "hs0", HC), ("hq1", "hs1", HC), ("oq", "osc", HC), ("aq", "asc", ARR), ("kq", "ks", TC), ("wq", "ws", XC)):
+        b[q] = ("sbuf", [128, w], "float8_e4m3fn_x4")
+        b[s] = ("sbuf", [128, w], "uint8")
+    for p in ("pd0", "pd1", "pd2", "pd3", "py0", "py1", "py2", "py3"):
+        b[p] = ("psum", [128, 512], "float32")
+    return b
+
+
+SCRATCH = _buffers()
+SEMAPHORES = ("lx0 lx1 lsnd lplc lqw lkc out arr sent ones idn ez0 ez eq qx0 qx1 conv hq0 hq1 oq wq kq0 kq1 pidx qq pad er ef eoff kneg vals kio vinit "
+              "ia ib ic ie it inv mo0 mo1 co0 co1 mk00 mk01 mk10 mk11 ck00 ck01 ck10 ck11 ma0 ma1 ca0 ca1 y00 y01 y10 y11 "
+              "m00 m01 m02 m03 m10 m11 m12 m13 c00 c01 c02 c03 c10 c11 c12 c13 g00 g01 g02 g03 g10 g11 g12 g13 go").split()
 
 
 def send_masks(core, dests, topo):
@@ -95,7 +50,7 @@ def rank_program(g, core, T, topo):
         return
     S = T.sem
     v, a, t, sy = g.vector, g.scalar, g.tensor, g.sync
-    COPY = ActivationFunctionType.Copy
+    COPY, IDENT = ActivationFunctionType.Copy, ActivationFunctionType.Identity
     A = AluOpType
 
     for h in range(2):
@@ -108,167 +63,195 @@ def rank_program(g, core, T, topo):
     sy.dma_start(T.kb[:], T.kc[:, :]).then_inc(S.lkc, 16)
 
     v.memset(T.ones[:], 1.0).then_inc(S.ones, 1)
-    g.wait_ge(S.ones, 1)
-    g.affine_select(T.ez[:], T.ones[:], [[-1, 516]], A.is_equal, 0.0, 3, 4).then_inc(S.ez, 1)
+    v.memset(T.ez[:], 0.0).then_inc(S.ez0, 1)
     g.iota(T.pidx[:], [[1, 1]], 0, 1).then_inc(S.pidx, 1)
-    g.iota(T.ktab[:], [[16, 16]], PAD + TC, 1, allow_small_or_imprecise_dtypes=True).then_inc(S.ktab, 1)
+    g.wait_ge(S.ones, 1)
+    g.affine_select(T.idn[:], T.ones[:], [[-1, 128]], A.is_equal, 0.0, 0, 1).then_inc(S.idn, 1)
+    g.iota(T.kio[:], [[1, VI]], 0, 0, allow_small_or_imprecise_dtypes=True).then_inc(S.kio, 1)
+    g.iota(T.kneg[:], [[-16, 16]], -VI, -1).then_inc(S.kneg, 1)
     cut = CAPP * (rank + 1)
     nv = 1
     g.iota(T.vals[:, 0:cut], [[1, cut]], TC + XC - cut, 0, allow_small_or_imprecise_dtypes=True).then_inc(S.vals, 1)
     if cut < XC:
         g.iota(T.vals[:, cut:XC], [[1, XC - cut]], TC, 0, allow_small_or_imprecise_dtypes=True).then_inc(S.vals, 1)
         nv = 2
-    g.iota(T.vl[:, 0:544], [[1, 544]], -PAD, 0, allow_small_or_imprecise_dtypes=True).then_inc(S.vinit, 1)
 
+    v.wait_ge(S.pidx, 1)
+    v.tensor_scalar(T.q15[:], T.pidx[:], 15, None, A.bitwise_and).then_inc(S.qq, 1)
+    v.tensor_scalar(T.q16[:], T.pidx[:], 16, None, A.bitwise_and).then_inc(S.qq, 1)
+    v.wait_ge(S.idn, 1)
+    v.wait_ge(S.ez0, 1)
+    v.tensor_copy(T.ez[:, 3:515:4], T.idn[:]).then_inc(S.ez, 1)
+    v.wait_ge(S.qq, 2)
+    v.tensor_scalar(T.padb[:], T.q16[:], 16.0, None, A.subtract).then_inc(S.pad, 1)
+    v.tensor_scalar(T.padc[:], T.q16[:], -1.0, 16.0, A.mult, A.add).then_inc(S.pad, 1)
+    v.tensor_scalar(T.er[:], T.q15[:], 16.0, 16.0, A.mult, A.add).then_inc(S.er, 1)
     v.wait_ge(S.ez, 1)
     for b in range(4):
         v.quantize_mx(T.eq[:, 128 * b:128 * b + 128], T.es[:, 128 * b:128 * b + 128],
                       T.ez[:, 3 - b:3 - b + 512]).then_inc(S.eq, 1)
-    v.wait_ge(S.pidx, 1)
-    v.tensor_scalar(T.pand[:], T.pidx[:], 16, None, A.bitwise_and).then_inc(S.pand, 1)
-    v.wait_ge(S.pand, 1)
-    v.tensor_scalar(T.mlo[:], T.pand[:], 0.0, None, A.is_equal).then_inc(S.mask, 1)
-    v.tensor_scalar(T.mhi[:], T.pand[:], 0.0, None, A.is_gt).then_inc(S.mask, 1)
+    v.wait_ge(S.er, 1)
+    v.tensor_tensor(T.ef[:], T.er[:], T.q16[:], A.subtract).then_inc(S.ef, 1)
+    v.wait_ge(S.ef, 1)
+    v.tensor_copy(T.eoff[:, 0:1], T.ef[:]).then_inc(S.eoff, 1)
+    v.tensor_scalar(T.eoff[:, 1:2], T.ef[:], 256.0, None, A.add).then_inc(S.eoff, 1)
+    a.wait_ge(S.kio, 1)
+    a.wait_ge(S.pad, 2)
+    a.activation(T.vl[:, 0:VI], T.kio[:], IDENT, bias=T.padb[:, 0:1]).then_inc(S.vinit, 1)
 
-    for h in range(2):
+    def quant_x(h):
         v.wait_ge(S["lx%d" % h], 16)
         v.quantize_mx(T.xq[:, HC * h:HC * h + HC], T.xs[:, HC * h:HC * h + HC],
                       T.xb[:, 512 * h:512 * h + 512]).then_inc(S["qx%d" % h], 1)
-    bank = {(0, 0): "pd0", (0, 1): "pd1", (0, 2): "pd2", (0, 3): "pd3",
-            (1, 0): "pd4", (1, 1): "pd5", (1, 2): "pd0", (1, 3): "pd1"}
+    quant_x(0)
     t.wait_ge(S.eq, 4)
     for h in range(2):
         t.wait_ge(S["qx%d" % h], 1)
         for b in range(4):
-            if (h, b) == (1, 2):
-                t.wait_ge(S.c00, 1)
-            if (h, b) == (1, 3):
-                t.wait_ge(S.c01, 1)
-            t.matmul_mx(T[bank[h, b]][:, 0:HC], T.eq[:, 128 * b:128 * b + 128], T.es[:, 128 * b:128 * b + 128],
+            if h:
+                t.wait_ge(S["c0%d" % b], 1)
+            t.matmul_mx(T["pd%d" % b][:, 0:HC], T.eq[:, 128 * b:128 * b + 128], T.es[:, 128 * b:128 * b + 128],
                         T.xq[:, HC * h:HC * h + HC], T.xs[:, HC * h:HC * h + HC], True, True).then_inc(S["m%d%d" % (h, b)], 1)
+    c0 = 2 * (rank + 1)
+    nc = 1
     for h in range(2):
         for b in (0, 2):
             v.wait_ge(S["m%d%d" % (h, b)], 1)
-            v.tensor_copy(T["xd%d" % b][:, HC * h:HC * h + HC], T[bank[h, b]][:, 0:HC]).then_inc(S["c%d%d" % (h, b)], 1)
+            v.tensor_copy(T["xd%d" % b][:, HC * h:HC * h + HC], T["pd%d" % b][:, 0:HC]).then_inc(S["c%d%d" % (h, b)], 1)
+            if h == 0 and b == 0:
+                quant_x(1)
         for b in (1, 3):
             a.wait_ge(S["m%d%d" % (h, b)], 1)
-            a.activation(T["xd%d" % b][:, HC * h:HC * h + HC], T[bank[h, b]][:, 0:HC], COPY).then_inc(S["c%d%d" % (h, b)], 1)
+            a.activation(T["xd%d" % b][:, HC * h:HC * h + HC], T["pd%d" % b][:, 0:HC], COPY).then_inc(S["c%d%d" % (h, b)], 1)
         if h == 0:
             v.wait_ge(S.lsnd, 128)
-            v.tensor_copy(T.so[:], T.sl[:]).then_inc(S.conv, 1)
+            if c0 < 16:
+                v.tensor_copy(T.so[:, 0:16 - c0], T.sl[:, c0:16]).then_inc(S.conv, 1)
+                nc = 2
+            v.tensor_copy(T.so[:, 16 - c0:16], T.sl[:, 0:c0]).then_inc(S.conv, 1)
 
-    v.wait_ge(S.conv, 1)
-    for b in (0, 2):
-        v.wait_ge(S["c0%d" % b], 1)
-        v.wait_ge(S["c1%d" % b], 1)
-        v.tensor_copy(T.hb[:, b:4 * XC:4], T["xd%d" % b][:, 0:XC].indirect(T.so[:, 0:16])).then_inc(S["g%d" % b], 1)
-    a.wait_ge(S.conv, 1)
+    def pick(q, b, lo, n, sem):
+        out, win = T.hb[:, 4 * lo + b:4 * (lo + n):4], T["xd%d" % b][:, 0:XC].indirect(T.so[:, lo // 16:(lo + n) // 16])
+        if q is v:
+            v.tensor_copy(out, win).then_inc(S[sem], 1)
+        else:
+            a.activation(out, win, COPY).then_inc(S[sem], 1)
+
+    def quant_h(h):
+        for b in range(4):
+            v.wait_ge(S["g%d%d" % (h, b)], 1)
+        lo = SECOND * h
+        v.quantize_mx(T["hq%d" % h][:], T["hs%d" % h][:], T.hb[:, 4 * lo:4 * (lo + HC)]).then_inc(S["hq%d" % h], 1)
+
+    for q in (v, a):
+        q.wait_ge(S.conv, nc)
+        for b in ((0, 2) if q is v else (1, 3)):
+            q.wait_ge(S["c0%d" % b], 1)
+            q.wait_ge(S["c1%d" % b], 1)
+            pick(q, b, 0, HC, "g0%d" % b)
     for b in (1, 3):
+        pick(a, b, HC, SECOND, "g1%d" % b)
+    quant_h(0)
+    for b in (0, 2):
+        pick(v, b, HC, SECOND, "g1%d" % b)
+    quant_h(1)
+    for b in (0, 2):
         a.wait_ge(S["c0%d" % b], 1)
         a.wait_ge(S["c1%d" % b], 1)
-        a.activation(T.hb[:, b:4 * XC:4], T["xd%d" % b][:, 0:XC].indirect(T.so[:, 0:16]), COPY).then_inc(S["g%d" % b], 1)
     for b in range(4):
-        v.wait_ge(S["g%d" % b], 1)
-    v.quantize_mx(T.hq[:], T.hs[:], T.hb[:]).then_inc(S.hq, 1)
+        pick(a, b, ARR, CAPP, "go")
 
-    dests = [c for c in T.cores if c != core]
-    masks = send_masks(core, dests, topo)
-    g.wait_ge(S.hq, 1)
-    for planes in (False, True):
+    masks = send_masks(core, [c for c in T.cores if c != core], topo)
+    for planes, js in CALLS:
+        if not planes:
+            g.wait_ge(S["hq%d" % (js[0] // 4)], 1)
         tr = []
-        for j in range(1, N):
-            d = (rank + j) % N
-            dst = T.cores[d]
-            k = (rank - d - 1) % N
+        for j in js:
+            dst = T.cores[(rank + 1 + j) % N]
+            k = N - 2 - j
             rid, pid = topo.addr(dst)[:2]
+            h = j // 4
+            lo = CAPP * j - SECOND * h
             if planes:
-                src, out = T.hs[:, CAPP * d:CAPP * d + CAPP], T.asc[:, CAPP * k:CAPP * k + CAPP]
+                src, out = T["hs%d" % h][:, lo:lo + CAPP], T.asc[:, CAPP * k:CAPP * k + CAPP]
             else:
-                src = T.hq[:, CAPP * d:CAPP * d + CAPP].bitcast(dt.uint8)
+                src = T["hq%d" % h][:, lo:lo + CAPP].bitcast(dt.uint8)
                 out = T.aq[:, CAPP * k:CAPP * k + CAPP].bitcast(dt.uint8)
             tr.append(RemoteDMATransfer(dst_ids=[DstId(rid=rid, pnc=pid)], dma_engine_mask=masks[dst],
                                         remote_sem=S.arr, srcs=[src], dsts=[out]))
         g.remote_dma_fused(tr, local_sem=S.sent)
 
     v.wait_ge(S.lplc, 128)
-    v.tensor_scalar(T.neg[:], T.pl[:], 0.0, None, A.is_lt).then_inc(S.ia, 1)
-    v.tensor_scalar(T.p16[:], T.pl[:], float(PAD), None, A.add).then_inc(S.ia, 1)
+    v.wait_ge(S.kneg, 1)
+    v.tensor_tensor(T.nk[:], T.pl[:], T.kneg[:], A.mult).then_inc(S.ia, 1)
     v.wait_ge(S.lqw, 16)
     v.quantize_mx(T.wq[:], T.ws[:], T.qb[:]).then_inc(S.wq, 1)
-    v.wait_ge(S.ia, 2)
-    v.wait_ge(S.ktab, 1)
-    v.tensor_tensor(T.nk[:], T.neg[:], T.ktab[:], A.mult).then_inc(S.ib, 1)
+    v.wait_ge(S.ia, 1)
+    v.tensor_tensor(T.pm[:], T.nk[:], T.pl[:], A.max).then_inc(S.ib, 1)
     v.wait_ge(S.lkc, 16)
-    v.quantize_mx(T.kq[:], T.ks[:], T.kb[:]).then_inc(S.kq, 1)
+    v.quantize_mx(T.kq[:, 0:256], T.ks[:, 0:256], T.kb[:, 0:1024]).then_inc(S.kq0, 1)
     v.wait_ge(S.ib, 1)
-    v.tensor_tensor(T.pf[:], T.nk[:], T.p16[:], A.max).then_inc(S.ic, 1)
+    v.wait_ge(S.pad, 2)
+    v.tensor_scalar(T.po[:], T.pm[:], T.padc[:, 0:1], None, A.add).then_inc(S.ic, 1)
+    v.wait_ge(S.go, 4)
+    v.quantize_mx(T.oq[:], T.osc[:], T.hb[:, 4 * HC:4 * XC]).then_inc(S.oq, 1)
+    v.quantize_mx(T.kq[:, 256:512], T.ks[:, 256:512], T.kb[:, 1024:2048]).then_inc(S.kq1, 1)
     v.wait_ge(S.ic, 1)
-    v.tensor_copy(T.po[:], T.pf[:]).then_inc(S.id, 1)
-    v.wait_ge(S.id, 1)
     v.wait_ge(S.vals, nv)
     v.wait_ge(S.vinit, 1)
     v.tensor_copy(T.vl[:, 0:VW].indirect(T.po[:, 0:16]), T.vals[:, 0:XC]).then_inc(S.ie, 1)
     v.wait_ge(S.ie, 1)
-    v.transpose(T.t1[:], T.vl[:, PAD:PAD + 512]).then_inc(S.it, 1)
-    v.transpose(T.t2[:], T.vl[:, 0:544]).then_inc(S.it, 1)
-    v.wait_ge(S.it, 2)
-    v.wait_ge(S.mask, 2)
-    v.tensor_scalar(T.u1[:, 0:32:2], T.t1[:, 0:512:32], T.mlo[:, 0:1], None, A.mult).then_inc(S.ig, 1)
-    v.tensor_scalar(T.u1[:, 1:32:2], T.t1[:, 0:512:32], T.mhi[:, 0:1], None, A.mult).then_inc(S.ig, 1)
-    v.tensor_scalar(T.u2[:, 0:32:2], T.t2[:, 0:512:32], T.mhi[:, 0:1], None, A.mult).then_inc(S.ig, 1)
-    v.tensor_scalar(T.u2[:, 1:32:2], T.t2[:, 32:544:32], T.mlo[:, 0:1], None, A.mult).then_inc(S.ig, 1)
-    v.wait_ge(S.ig, 4)
-    v.tensor_tensor(T.inf32[:], T.u1[:], T.u2[:], A.add).then_inc(S.ih, 1)
-    v.wait_ge(S.ih, 1)
-    v.tensor_copy(T.inv[:], T.inf32[:]).then_inc(S.inv, 1)
+    v.transpose(T.tr[:], T.vl[:, 0:VI]).then_inc(S.it, 1)
+    v.wait_ge(S.it, 1)
+    v.wait_ge(S.eoff, 2)
+    v.tensor_copy(T.inv[:], T.tr[:, 0:VI].indirect(T.eoff[:, 0:2])).then_inc(S.inv, 1)
 
-    w = min(CAPP * rank, XC - 128)
-    own = CAPP * rank - w
+    def product(bank, o, q, s, n, sem):
+        t.matmul_mx(T[bank][:, 0:n], T.wq[:, 128 * o:128 * o + 128], T.ws[:, 128 * o:128 * o + 128], q, s, True, True).then_inc(S[sem], 1)
     t.wait_ge(S.wq, 1)
-    t.wait_ge(S.hq, 1)
+    t.wait_ge(S.kq0, 1)
     for o in range(2):
-        t.matmul_mx(T["py%d" % o][:, 0:128], T.wq[:, 128 * o:128 * o + 128], T.ws[:, 128 * o:128 * o + 128],
-                    T.hq[:, w:w + 128], T.hs[:, w:w + 128], True, True).then_inc(S["mo%d" % o], 1)
+        product("py%d" % o, o, T.kq[:, 0:256], T.ks[:, 0:256], 256, "mk0%d" % o)
+    t.wait_ge(S.oq, 1)
     for o in range(2):
-        a.wait_ge(S["mo%d" % o], 1)
-        a.activation(T["w%d" % o][:, TC + ARR:TC + XC], T["py%d" % o][:, own:own + CAPP], COPY).then_inc(S["co%d" % o], 1)
-    t.wait_ge(S.kq, 1)
+        product("py%d" % (2 + o), o, T.oq[:], T.osc[:], HC, "mo%d" % o)
+    t.wait_ge(S.kq1, 1)
     for o in range(2):
         t.wait_ge(S["co%d" % o], 1)
-        t.matmul_mx(T["py%d" % o][:, 0:TC], T.wq[:, 128 * o:128 * o + 128], T.ws[:, 128 * o:128 * o + 128],
-                    T.kq[:], T.ks[:], True, True).then_inc(S["mk%d" % o], 1)
+        product("py%d" % (2 + o), o, T.kq[:, 256:512], T.ks[:, 256:512], 256, "mk1%d" % o)
     for o in range(2):
-        a.wait_ge(S["mk%d" % o], 1)
-        a.activation(T["w%d" % o][:, 0:TC], T["py%d" % o][:, 0:TC], COPY).then_inc(S["ck%d" % o], 1)
+        a.wait_ge(S["mk0%d" % o], 1)
+        a.activation(T["w%d" % o][:, 0:256], T["py%d" % o][:, 0:256], COPY).then_inc(S["ck0%d" % o], 1)
+    for o in range(2):
+        a.wait_ge(S["mo%d" % o], 1)
+        a.activation(T["w%d" % o][:, TC + ARR:TC + XC], T["py%d" % (2 + o)][:, HC - CAPP:HC], COPY).then_inc(S["co%d" % o], 1)
+    for o in range(2):
+        a.wait_ge(S["mk1%d" % o], 1)
+        a.activation(T["w%d" % o][:, 256:512], T["py%d" % (2 + o)][:, 0:256], COPY).then_inc(S["ck1%d" % o], 1)
 
     for o in range(2):
-        t.wait_ge(S["ck%d" % o], 1)
+        t.wait_ge(S["ck0%d" % o], 1)
     t.wait_ge(S.arr, 2 * 2 * (N - 1))
     for o in range(2):
-        t.matmul_mx(T["py%d" % o][:, 0:ARR], T.wq[:, 128 * o:128 * o + 128], T.ws[:, 128 * o:128 * o + 128],
-                    T.aq[:], T.asc[:], True, True).then_inc(S["ma%d" % o], 1)
+        product("py%d" % o, o, T.aq[:], T.asc[:], ARR, "ma%d" % o)
 
     v.wait_ge(S.ma0, 1)
     v.tensor_copy(T.w0[:, TC:TC + ARR], T.py0[:, 0:ARR]).then_inc(S.ca0, 1)
-    v.wait_ge(S.ca0, 1)
-    v.wait_ge(S.co0, 1)
-    v.wait_ge(S.ck0, 1)
-    v.wait_ge(S.inv, 1)
     a.wait_ge(S.ma1, 1)
     a.activation(T.w1[:, TC:TC + ARR], T.py1[:, 0:ARR], COPY).then_inc(S.ca1, 1)
-    a.wait_ge(S.ca1, 1)
-    a.wait_ge(S.co1, 1)
-    a.wait_ge(S.ck1, 1)
-    a.wait_ge(S.inv, 1)
-    for h in range(2):
-        v.tensor_copy(T.y0[:, 256 * h:256 * h + 256],
-                      T.w0[:, 0:TC + XC].indirect(T.inv[:, 16 * h:16 * h + 16])).then_inc(S["y0%d" % h], 1)
-        a.activation(T.y1[:, 256 * h:256 * h + 256],
-                     T.w1[:, 0:TC + XC].indirect(T.inv[:, 16 * h:16 * h + 16]), COPY).then_inc(S["y1%d" % h], 1)
-    for h in range(2):
+    for o, q in ((0, v), (1, a)):
+        for s in ("co%d", "ck0%d", "ck1%d", "ca%d"):
+            q.wait_ge(S[s % o], 1)
+        q.wait_ge(S.inv, 1)
+        for i, (at, n) in enumerate(YP):
+            out, win = T["y%d" % o][:, at:at + n], T["w%d" % o][:, 0:TC + XC].indirect(T.inv[:, at // 16:(at + n) // 16])
+            if q is v:
+                v.tensor_copy(out, win).then_inc(S["y%d%d" % (o, i)], 1)
+            else:
+                a.activation(out, win, COPY).then_inc(S["y%d%d" % (o, i)], 1)
+    for i, (at, n) in enumerate(YP):
         for o in range(2):
-            sy.wait_ge(S["y%d%d" % (o, h)], 1)
-            sy.dma_start(T.y[:, TC * o + 256 * h:TC * o + 256 * h + 256],
-                         T["y%d" % o][:, 256 * h:256 * h + 256]).then_inc(S.out, 16)
-    sy.wait_ge(S.out, 64)
+            sy.wait_ge(S["y%d%d" % (o, i)], 1)
+            sy.dma_start(T.y[:, TC * o + at:TC * o + at + n], T["y%d" % o][:, at:at + n]).then_inc(S.out, 16)
+    sy.wait_ge(S.out, 16 * 2 * len(YP))
     g.wait_ge(S.sent, 2 * 2 * (N - 1))

@@ -2,24 +2,27 @@ from concourse.bass import DstId, RemoteDMATransfer
 from concourse.mybir import dt, AluOpType, ActivationFunctionType
 
 N, CAPP, XC, HC, TC = 8, 32, 256, 128, 512
+HALF = N // 2
 ARR = (N - 1) * CAPP
 VI = TC + 32
 VW = VI + 368
+FAR = 1024
 YP = ((0, 192), (192, 320))
-SECOND = ARR - HC
-CALLS = ((False, (0, 1, 2, 3)), (False, (4, 5, 6)), (True, (0, 1, 2, 3, 4, 5, 6)))
+CALLS = ((False, (0,)), (False, (1,)), (True, (0, 1)))
+VSTEPS = "e0 e1 t x0 e2 e3 c00 x1 c02 o c10 c12 p00 p02 p10 h0 p12 h1"
+ASTEPS = "c01 c03 c11 c13 p01 p03 p11 p13 f j"
 
 
 def _buffers():
     b = {}
-    for dtype, names in (("bfloat16", {"xb": 1024, "kb": 2048, "qb": 1024, "ones": 128, "idn": 128, "ez": 516, "xd0": XC, "xd1": XC, "xd2": XC, "xd3": XC, "hb": 1024}),
-                         ("int32", {"sl": 16, "pl": 16, "pidx": 1, "q15": 1, "q16": 1, "kneg": 16}),
+    for dtype, names in (("bfloat16", {"xb": 1024, "kb": 2048, "qb": 1024, "dg": 128, "ez": VI, "xd0": XC, "xd1": XC, "xd2": XC, "xd3": XC, "hb0": 512, "hb1": 512,
+                                       "vals": XC, "vl": VW, "tr": VI, "tab": 128, "tabt": 128}),
+                         ("int32", {"sl": 16, "pl": 16, "kneg": 16}),
                          ("uint16", {"so": 16, "po": 16, "inv": 32, "eoff": 2}),
-                         ("float32", {"padc": 1, "padb": 1, "er": 1, "ef": 1, "vals": XC, "kio": VI, "vl": VW, "nk": 16, "pm": 16, "tr": VI,
-                                      "w0": TC + XC, "w1": TC + XC, "y0": TC, "y1": TC})):
+                         ("float32", {"far": 1, "nk": 16, "pm": 16, "jc": 32, "jt": 32, "sf": 32, "w0": TC + XC, "w1": TC + XC, "y0": TC, "y1": TC})):
         for k, w in names.items():
             b[k] = ("sbuf", [128, w], dtype)
-    for q, s, w in (("eq", "es", 512), ("xq", "xs", XC), ("hq0", "hs0", HC), ("hq1", "hs1", HC), ("oq", "osc", HC), ("aq", "asc", ARR), ("kq", "ks", TC), ("wq", "ws", XC)):
+    for q, s, w in (("eq", "es", 512), ("xq", "xs", XC), ("hq0", "hs0", HC), ("hq1", "hs1", HC), ("aq", "asc", ARR), ("kq", "ks", TC), ("wq", "ws", XC)):
         b[q] = ("sbuf", [128, w], "float8_e4m3fn_x4")
         b[s] = ("sbuf", [128, w], "uint8")
     for p in ("pd0", "pd1", "pd2", "pd3", "py0", "py1", "py2", "py3"):
@@ -28,9 +31,9 @@ def _buffers():
 
 
 SCRATCH = _buffers()
-SEMAPHORES = ("lx0 lx1 lsnd lplc lqw lkc out arr sent ones idn ez0 ez eq qx0 qx1 conv hq0 hq1 oq wq kq0 kq1 pidx qq pad er ef eoff kneg vals kio vinit "
-              "ia ib ic ie it inv mo0 mo1 co0 co1 mk00 mk01 mk10 mk11 ck00 ck01 ck10 ck11 ma0 ma1 ca0 ca1 y00 y01 y10 y11 "
-              "m00 m01 m02 m03 m10 m11 m12 m13 c00 c01 c02 c03 c10 c11 c12 c13 g00 g01 g02 g03 g10 g11 g12 g13 go").split()
+SEMAPHORES = ("lx0 lx1 lsnd lplc lqw lkc out arr sent dg far ez0 ez eq0 eq1 eq2 eq3 qx0 qx1 conv hq0 hq1 wq kq0 kq1 tab tabt eoff kneg vals jc jt vinit "
+              "ia ib ic ie it iu inv mo0 mo1 co0 co1 mk00 mk01 mk10 mk11 ck00 ck01 ck10 ck11 ma0 ma1 ca0 ca1 y00 y01 y10 y11 "
+              "m00 m01 m02 m03 m10 m11 m12 m13 c00 c01 c02 c03 c10 c11 c12 c13 g00 g01 g02 g03 g10 g11 g12 g13").split()
 
 
 def send_masks(core, dests, topo):
@@ -52,6 +55,14 @@ def rank_program(g, core, T, topo):
     v, a, t, sy = g.vector, g.scalar, g.tensor, g.sync
     COPY, IDENT = ActivationFunctionType.Copy, ActivationFunctionType.Identity
     A = AluOpType
+    half, pos = rank // HALF, rank % HALF
+    halves = (1 - half, half)
+
+    def copy(q, out, win, sem):
+        if q is v:
+            v.tensor_copy(out, win).then_inc(S[sem], 1)
+        else:
+            a.activation(out, win, COPY).then_inc(S[sem], 1)
 
     for h in range(2):
         sy.dma_start(T.xb[:, 512 * h:512 * h + 512], T.x[:, 512 * h:512 * h + 512]).then_inc(S["lx%d" % h], 16)
@@ -62,123 +73,108 @@ def rank_program(g, core, T, topo):
     sy.dma_start(T.qb[:], T.qw[:, :]).then_inc(S.lqw, 16)
     sy.dma_start(T.kb[:], T.kc[:, :]).then_inc(S.lkc, 16)
 
-    v.memset(T.ones[:], 1.0).then_inc(S.ones, 1)
+    g.iota(T.dg[:], [[-1, 128]], 0, 1, allow_small_or_imprecise_dtypes=True).then_inc(S.dg, 1)
     v.memset(T.ez[:], 0.0).then_inc(S.ez0, 1)
-    g.iota(T.pidx[:], [[1, 1]], 0, 1).then_inc(S.pidx, 1)
-    g.wait_ge(S.ones, 1)
-    g.affine_select(T.idn[:], T.ones[:], [[-1, 128]], A.is_equal, 0.0, 0, 1).then_inc(S.idn, 1)
-    g.iota(T.kio[:], [[1, VI]], 0, 0, allow_small_or_imprecise_dtypes=True).then_inc(S.kio, 1)
-    g.iota(T.kneg[:], [[-16, 16]], -VI, -1).then_inc(S.kneg, 1)
-    cut = CAPP * (rank + 1)
-    nv = 1
-    g.iota(T.vals[:, 0:cut], [[1, cut]], TC + XC - cut, 0, allow_small_or_imprecise_dtypes=True).then_inc(S.vals, 1)
-    if cut < XC:
-        g.iota(T.vals[:, cut:XC], [[1, XC - cut]], TC, 0, allow_small_or_imprecise_dtypes=True).then_inc(S.vals, 1)
-        nv = 2
-
-    v.wait_ge(S.pidx, 1)
-    v.tensor_scalar(T.q15[:], T.pidx[:], 15, None, A.bitwise_and).then_inc(S.qq, 1)
-    v.tensor_scalar(T.q16[:], T.pidx[:], 16, None, A.bitwise_and).then_inc(S.qq, 1)
-    v.wait_ge(S.idn, 1)
+    v.wait_ge(S.dg, 1)
     v.wait_ge(S.ez0, 1)
-    v.tensor_copy(T.ez[:, 3:515:4], T.idn[:]).then_inc(S.ez, 1)
-    v.wait_ge(S.qq, 2)
-    v.tensor_scalar(T.padb[:], T.q16[:], 16.0, None, A.subtract).then_inc(S.pad, 1)
-    v.tensor_scalar(T.padc[:], T.q16[:], -1.0, 16.0, A.mult, A.add).then_inc(S.pad, 1)
-    v.tensor_scalar(T.er[:], T.q15[:], 16.0, 16.0, A.mult, A.add).then_inc(S.er, 1)
-    v.wait_ge(S.ez, 1)
-    for b in range(4):
-        v.quantize_mx(T.eq[:, 128 * b:128 * b + 128], T.es[:, 128 * b:128 * b + 128],
-                      T.ez[:, 3 - b:3 - b + 512]).then_inc(S.eq, 1)
-    v.wait_ge(S.er, 1)
-    v.tensor_tensor(T.ef[:], T.er[:], T.q16[:], A.subtract).then_inc(S.ef, 1)
-    v.wait_ge(S.ef, 1)
-    v.tensor_copy(T.eoff[:, 0:1], T.ef[:]).then_inc(S.eoff, 1)
-    v.tensor_scalar(T.eoff[:, 1:2], T.ef[:], 256.0, None, A.add).then_inc(S.eoff, 1)
-    a.wait_ge(S.kio, 1)
-    a.wait_ge(S.pad, 2)
-    a.activation(T.vl[:, 0:VI], T.kio[:], IDENT, bias=T.padb[:, 0:1]).then_inc(S.vinit, 1)
+    v.tensor_scalar(T.ez[:, 3:515:4], T.dg[:], 0.0, None, A.is_equal).then_inc(S.ez, 1)
+    g.iota(T.tab[:, 0:64], [[256, 2], [-16, 2], [16, 16]], 16, 0, allow_small_or_imprecise_dtypes=True).then_inc(S.tab, 1)
+    g.iota(T.tab[:, 64:96], [[-16, 2], [0, 16]], 16, 0, allow_small_or_imprecise_dtypes=True).then_inc(S.tab, 1)
+    g.iota(T.tab[:, 96:128], [[0, 2], [1, 16]], 0, 0, allow_small_or_imprecise_dtypes=True).then_inc(S.tab, 1)
+    g.iota(T.far[:], [[0, 1]], FAR, 0, allow_small_or_imprecise_dtypes=True).then_inc(S.far, 1)
+    g.iota(T.jc[:], [[16, 32]], XC, 0, allow_small_or_imprecise_dtypes=True).then_inc(S.jc, 1)
+    g.iota(T.kneg[:], [[-16, 16]], -VI, -1).then_inc(S.kneg, 1)
+    nv = 0
+    for at, n, base in ((HC * halves[0], HC, 0), (HC * half, CAPP * pos, HC), (CAPP * rank, CAPP, ARR),
+                        (CAPP * rank + CAPP, HC - CAPP * pos - CAPP, HC + CAPP * pos)):
+        if n:
+            g.iota(T.vals[:, at:at + n], [[1, n]], base, 0, allow_small_or_imprecise_dtypes=True).then_inc(S.vals, 1)
+            nv += 1
+
+    def quant_e(b):
+        v.wait_ge(S.ez, 1)
+        v.quantize_mx(T.eq[:, 128 * b:128 * b + 128], T.es[:, 128 * b:128 * b + 128], T.ez[:, 3 - b:3 - b + 512]).then_inc(S["eq%d" % b], 1)
 
     def quant_x(h):
         v.wait_ge(S["lx%d" % h], 16)
         v.quantize_mx(T.xq[:, HC * h:HC * h + HC], T.xs[:, HC * h:HC * h + HC],
                       T.xb[:, 512 * h:512 * h + 512]).then_inc(S["qx%d" % h], 1)
-    quant_x(0)
-    t.wait_ge(S.eq, 4)
+
+    def tables():
+        v.wait_ge(S.tab, 3)
+        v.transpose(T.tabt[:], T.tab[:]).then_inc(S.tabt, 1)
+
+    def unpack(q, h, b):
+        q.wait_ge(S["m%d%d" % (h, b)], 1)
+        copy(q, T["xd%d" % b][:, HC * h:HC * h + HC], T[("pd%d", "py%d")[h] % b][:, 0:HC], "c%d%d" % (h, b))
+
+    def offsets():
+        v.wait_ge(S.lsnd, 128)
+        v.tensor_copy(T.so[:], T.sl[:]).then_inc(S.conv, 1)
+
+    def pick(q, ph, b):
+        q.wait_ge(S.conv, 1)
+        q.wait_ge(S["c0%d" % b], 1)
+        q.wait_ge(S["c1%d" % b], 1)
+        c = 2 * HALF * halves[ph]
+        copy(q, T["hb%d" % ph][:, b:512:4], T["xd%d" % b][:, 0:XC].indirect(T.so[:, c:c + 2 * HALF]), "g%d%d" % (ph, b))
+
+    def quant_h(ph):
+        for b in range(4):
+            v.wait_ge(S["g%d%d" % (ph, b)], 1)
+        v.quantize_mx(T["hq%d" % ph][:], T["hs%d" % ph][:], T["hb%d" % ph][:]).then_inc(S["hq%d" % ph], 1)
+
     for h in range(2):
         t.wait_ge(S["qx%d" % h], 1)
         for b in range(4):
-            if h:
-                t.wait_ge(S["c0%d" % b], 1)
-            t.matmul_mx(T["pd%d" % b][:, 0:HC], T.eq[:, 128 * b:128 * b + 128], T.es[:, 128 * b:128 * b + 128],
+            t.wait_ge(S["eq%d" % b], 1)
+            t.matmul_mx(T[("pd%d", "py%d")[h] % b][:, 0:HC], T.eq[:, 128 * b:128 * b + 128], T.es[:, 128 * b:128 * b + 128],
                         T.xq[:, HC * h:HC * h + HC], T.xs[:, HC * h:HC * h + HC], True, True).then_inc(S["m%d%d" % (h, b)], 1)
-    c0 = 2 * (rank + 1)
-    nc = 1
-    for h in range(2):
-        for b in (0, 2):
-            v.wait_ge(S["m%d%d" % (h, b)], 1)
-            v.tensor_copy(T["xd%d" % b][:, HC * h:HC * h + HC], T["pd%d" % b][:, 0:HC]).then_inc(S["c%d%d" % (h, b)], 1)
-            if h == 0 and b == 0:
-                quant_x(1)
-        for b in (1, 3):
-            a.wait_ge(S["m%d%d" % (h, b)], 1)
-            a.activation(T["xd%d" % b][:, HC * h:HC * h + HC], T["pd%d" % b][:, 0:HC], COPY).then_inc(S["c%d%d" % (h, b)], 1)
-        if h == 0:
-            v.wait_ge(S.lsnd, 128)
-            if c0 < 16:
-                v.tensor_copy(T.so[:, 0:16 - c0], T.sl[:, c0:16]).then_inc(S.conv, 1)
-                nc = 2
-            v.tensor_copy(T.so[:, 16 - c0:16], T.sl[:, 0:c0]).then_inc(S.conv, 1)
-
-    def pick(q, b, lo, n, sem):
-        out, win = T.hb[:, 4 * lo + b:4 * (lo + n):4], T["xd%d" % b][:, 0:XC].indirect(T.so[:, lo // 16:(lo + n) // 16])
-        if q is v:
-            v.tensor_copy(out, win).then_inc(S[sem], 1)
-        else:
-            a.activation(out, win, COPY).then_inc(S[sem], 1)
-
-    def quant_h(h):
-        for b in range(4):
-            v.wait_ge(S["g%d%d" % (h, b)], 1)
-        lo = SECOND * h
-        v.quantize_mx(T["hq%d" % h][:], T["hs%d" % h][:], T.hb[:, 4 * lo:4 * (lo + HC)]).then_inc(S["hq%d" % h], 1)
-
-    for q in (v, a):
-        q.wait_ge(S.conv, nc)
-        for b in ((0, 2) if q is v else (1, 3)):
-            q.wait_ge(S["c0%d" % b], 1)
-            q.wait_ge(S["c1%d" % b], 1)
-            pick(q, b, 0, HC, "g0%d" % b)
-    for b in (1, 3):
-        pick(a, b, HC, SECOND, "g1%d" % b)
-    quant_h(0)
-    for b in (0, 2):
-        pick(v, b, HC, SECOND, "g1%d" % b)
-    quant_h(1)
-    for b in (0, 2):
-        a.wait_ge(S["c0%d" % b], 1)
-        a.wait_ge(S["c1%d" % b], 1)
-    for b in range(4):
-        pick(a, b, ARR, CAPP, "go")
+    for q, steps in ((v, VSTEPS), (a, ASTEPS)):
+        for w in steps.split():
+            n = [int(c) for c in w[1:]]
+            if w[0] == "e":
+                quant_e(*n)
+            elif w[0] == "t":
+                tables()
+            elif w[0] == "x":
+                quant_x(*n)
+            elif w[0] == "c":
+                unpack(q, *n)
+            elif w[0] == "o":
+                offsets()
+            elif w[0] == "p":
+                pick(q, *n)
+            elif w[0] == "h":
+                quant_h(*n)
+            elif w[0] == "f":
+                a.wait_ge(S.far, 1)
+                a.wait_ge(S.ez, 1)
+                a.activation(T.vl[:, 0:VI], T.ez[:], IDENT, bias=T.far[:, 0:1], scale=0.0).then_inc(S.vinit, 1)
+            else:
+                a.wait_ge(S.tabt, 1)
+                a.wait_ge(S.jc, 1)
+                a.activation(T.jt[:], T.jc[:], IDENT, bias=T.tabt[:, 96:97]).then_inc(S.jt, 1)
 
     masks = send_masks(core, [c for c in T.cores if c != core], topo)
-    for planes, js in CALLS:
-        if not planes:
-            g.wait_ge(S["hq%d" % (js[0] // 4)], 1)
+    for planes, parts in CALLS:
         tr = []
-        for j in js:
-            dst = T.cores[(rank + 1 + j) % N]
-            k = N - 2 - j
-            rid, pid = topo.addr(dst)[:2]
-            h = j // 4
-            lo = CAPP * j - SECOND * h
-            if planes:
-                src, out = T["hs%d" % h][:, lo:lo + CAPP], T.asc[:, CAPP * k:CAPP * k + CAPP]
-            else:
-                src = T["hq%d" % h][:, lo:lo + CAPP].bitcast(dt.uint8)
-                out = T.aq[:, CAPP * k:CAPP * k + CAPP].bitcast(dt.uint8)
-            tr.append(RemoteDMATransfer(dst_ids=[DstId(rid=rid, pnc=pid)], dma_engine_mask=masks[dst],
-                                        remote_sem=S.arr, srcs=[src], dsts=[out]))
+        for ph in parts:
+            g.wait_ge(S["hq%d" % ph], 1)
+            for k in range(HALF):
+                d = HALF * halves[ph] + k
+                if d == rank:
+                    continue
+                dst = T.cores[d]
+                rid, pid = topo.addr(dst)[:2]
+                lo = CAPP * k
+                at = HC * ph + CAPP * (pos - (1 if ph and rank > d else 0))
+                if planes:
+                    src, out = T["hs%d" % ph][:, lo:lo + CAPP], T.asc[:, at:at + CAPP]
+                else:
+                    src, out = T["hq%d" % ph][:, lo:lo + CAPP].bitcast(dt.uint8), T.aq[:, at:at + CAPP].bitcast(dt.uint8)
+                tr.append(RemoteDMATransfer(dst_ids=[DstId(rid=rid, pnc=pid)], dma_engine_mask=masks[dst],
+                                            remote_sem=S.arr, srcs=[src], dsts=[out]))
         g.remote_dma_fused(tr, local_sem=S.sent)
 
     v.wait_ge(S.lplc, 128)
@@ -191,64 +187,53 @@ def rank_program(g, core, T, topo):
     v.wait_ge(S.lkc, 16)
     v.quantize_mx(T.kq[:, 0:256], T.ks[:, 0:256], T.kb[:, 0:1024]).then_inc(S.kq0, 1)
     v.wait_ge(S.ib, 1)
-    v.wait_ge(S.pad, 2)
-    v.tensor_scalar(T.po[:], T.pm[:], T.padc[:, 0:1], None, A.add).then_inc(S.ic, 1)
-    v.wait_ge(S.go, 4)
-    v.quantize_mx(T.oq[:], T.osc[:], T.hb[:, 4 * HC:4 * XC]).then_inc(S.oq, 1)
+    v.wait_ge(S.tabt, 1)
+    v.tensor_scalar(T.po[:], T.pm[:], T.tabt[:, 64:65], None, A.add).then_inc(S.ic, 1)
     v.quantize_mx(T.kq[:, 256:512], T.ks[:, 256:512], T.kb[:, 1024:2048]).then_inc(S.kq1, 1)
     v.wait_ge(S.ic, 1)
     v.wait_ge(S.vals, nv)
     v.wait_ge(S.vinit, 1)
     v.tensor_copy(T.vl[:, 0:VW].indirect(T.po[:, 0:16]), T.vals[:, 0:XC]).then_inc(S.ie, 1)
+    v.tensor_copy(T.eoff[:], T.tabt[:, 0:64:32]).then_inc(S.eoff, 1)
     v.wait_ge(S.ie, 1)
     v.transpose(T.tr[:], T.vl[:, 0:VI]).then_inc(S.it, 1)
     v.wait_ge(S.it, 1)
-    v.wait_ge(S.eoff, 2)
-    v.tensor_copy(T.inv[:], T.tr[:, 0:VI].indirect(T.eoff[:, 0:2])).then_inc(S.inv, 1)
+    v.wait_ge(S.eoff, 1)
+    v.wait_ge(S.jt, 1)
+    v.tensor_tensor(T.sf[:], T.tr[:, 0:VI].indirect(T.eoff[:, 0:2]), T.jt[:], A.min).then_inc(S.iu, 1)
+    v.wait_ge(S.iu, 1)
+    v.tensor_copy(T.inv[:], T.sf[:]).then_inc(S.inv, 1)
 
     def product(bank, o, q, s, n, sem):
         t.matmul_mx(T[bank][:, 0:n], T.wq[:, 128 * o:128 * o + 128], T.ws[:, 128 * o:128 * o + 128], q, s, True, True).then_inc(S[sem], 1)
     t.wait_ge(S.wq, 1)
-    t.wait_ge(S.kq0, 1)
+    for h, bank in ((0, "py%d"), (1, "pd%d")):
+        t.wait_ge(S["kq%d" % h], 1)
+        for o in range(2):
+            t.wait_ge(S["c%d%d" % (1 - h, o)], 1)
+            product(bank % o, o, T.kq[:, 256 * h:256 * h + 256], T.ks[:, 256 * h:256 * h + 256], 256, "mk%d%d" % (h, o))
+            a.wait_ge(S["mk%d%d" % (h, o)], 1)
+            copy(a, T["w%d" % o][:, XC + 256 * h:XC + 256 * h + 256], T[bank % o][:, 0:256], "ck%d%d" % (h, o))
     for o in range(2):
-        product("py%d" % o, o, T.kq[:, 0:256], T.ks[:, 0:256], 256, "mk0%d" % o)
-    t.wait_ge(S.oq, 1)
-    for o in range(2):
-        product("py%d" % (2 + o), o, T.oq[:], T.osc[:], HC, "mo%d" % o)
-    t.wait_ge(S.kq1, 1)
-    for o in range(2):
-        t.wait_ge(S["co%d" % o], 1)
-        product("py%d" % (2 + o), o, T.kq[:, 256:512], T.ks[:, 256:512], 256, "mk1%d" % o)
-    for o in range(2):
-        a.wait_ge(S["mk0%d" % o], 1)
-        a.activation(T["w%d" % o][:, 0:256], T["py%d" % o][:, 0:256], COPY).then_inc(S["ck0%d" % o], 1)
-    for o in range(2):
+        bank = "py%d" % (2 + o)
+        t.wait_ge(S["c1%d" % (2 + o)], 1)
+        product(bank, o, T.hq1[:], T.hs1[:], HC, "mo%d" % o)
         a.wait_ge(S["mo%d" % o], 1)
-        a.activation(T["w%d" % o][:, TC + ARR:TC + XC], T["py%d" % (2 + o)][:, HC - CAPP:HC], COPY).then_inc(S["co%d" % o], 1)
-    for o in range(2):
-        a.wait_ge(S["mk1%d" % o], 1)
-        a.activation(T["w%d" % o][:, 256:512], T["py%d" % (2 + o)][:, 0:256], COPY).then_inc(S["ck1%d" % o], 1)
+        copy(a, T["w%d" % o][:, ARR:XC], T[bank][:, CAPP * pos:CAPP * pos + CAPP], "co%d" % o)
 
-    for o in range(2):
-        t.wait_ge(S["ck0%d" % o], 1)
     t.wait_ge(S.arr, 2 * 2 * (N - 1))
     for o in range(2):
-        product("py%d" % o, o, T.aq[:], T.asc[:], ARR, "ma%d" % o)
+        t.wait_ge(S["c0%d" % (2 + o)], 1)
+        product("pd%d" % (2 + o), o, T.aq[:], T.asc[:], ARR, "ma%d" % o)
 
-    v.wait_ge(S.ma0, 1)
-    v.tensor_copy(T.w0[:, TC:TC + ARR], T.py0[:, 0:ARR]).then_inc(S.ca0, 1)
-    a.wait_ge(S.ma1, 1)
-    a.activation(T.w1[:, TC:TC + ARR], T.py1[:, 0:ARR], COPY).then_inc(S.ca1, 1)
     for o, q in ((0, v), (1, a)):
+        q.wait_ge(S["ma%d" % o], 1)
+        copy(q, T["w%d" % o][:, 0:ARR], T["pd%d" % (2 + o)][:, 0:ARR], "ca%d" % o)
         for s in ("co%d", "ck0%d", "ck1%d", "ca%d"):
             q.wait_ge(S[s % o], 1)
         q.wait_ge(S.inv, 1)
         for i, (at, n) in enumerate(YP):
-            out, win = T["y%d" % o][:, at:at + n], T["w%d" % o][:, 0:TC + XC].indirect(T.inv[:, at // 16:(at + n) // 16])
-            if q is v:
-                v.tensor_copy(out, win).then_inc(S["y%d%d" % (o, i)], 1)
-            else:
-                a.activation(out, win, COPY).then_inc(S["y%d%d" % (o, i)], 1)
+            copy(q, T["y%d" % o][:, at:at + n], T["w%d" % o][:, 0:TC + XC].indirect(T.inv[:, at // 16:(at + n) // 16]), "y%d%d" % (o, i))
     for i, (at, n) in enumerate(YP):
         for o in range(2):
             sy.wait_ge(S["y%d%d" % (o, i)], 1)

from concourse.bass import DstId, RemoteDMATransfer
from concourse.mybir import dt, AluOpType, ActivationFunctionType

N, CAPP, XC, HC, TC = 8, 32, 256, 128, 512
HALF = N // 2
ARR = (N - 1) * CAPP
VI = TC + 32
VW = VI + 368
FAR = 1024
YP = ((0, 192), (192, 320))
CALLS = ((False, (0,)), (False, (1,)), (True, (0, 1)))
VSTEPS = "e0 e1 t x0 e2 e3 c00 x1 c02 o c10 c12 p00 p02 p10 h0 p12 h1"
ASTEPS = "c01 c03 c11 c13 p01 p03 p11 p13 f j"


def _buffers():
    b = {}
    for dtype, names in (("bfloat16", {"xb": 1024, "kb": 2048, "qb": 1024, "dg": 128, "ez": VI, "xd0": XC, "xd1": XC, "xd2": XC, "xd3": XC, "hb0": 512, "hb1": 512,
                                       "vals": XC, "vl": VW, "tr": VI, "tab": 128, "tabt": 128}),
                         ("int32", {"sl": 16, "pl": 16, "kneg": 16}),
                         ("uint16", {"so": 16, "po": 16, "inv": 32, "eoff": 2}),
                         ("float32", {"far": 1, "nk": 16, "pm": 16, "jc": 32, "jt": 32, "sf": 32, "w0": TC + XC, "w1": TC + XC, "y0": TC, "y1": TC})):
        for k, w in names.items():
            b[k] = ("sbuf", [128, w], dtype)
    for q, s, w in (("eq", "es", 512), ("xq", "xs", XC), ("hq0", "hs0", HC), ("hq1", "hs1", HC), ("aq", "asc", ARR), ("kq", "ks", TC), ("wq", "ws", XC)):
        b[q] = ("sbuf", [128, w], "float8_e4m3fn_x4")
        b[s] = ("sbuf", [128, w], "uint8")
    for p in ("pd0", "pd1", "pd2", "pd3", "py0", "py1", "py2", "py3"):
        b[p] = ("psum", [128, 512], "float32")
    return b


SCRATCH = _buffers()
SEMAPHORES = ("lx0 lx1 lsnd lplc lqw lkc out arr sent dg far ez0 ez eq0 eq1 eq2 eq3 qx0 qx1 conv hq0 hq1 wq kq0 kq1 tab tabt eoff kneg vals jc jt vinit "
              "ia ib ic ie it iu inv mo0 mo1 co0 co1 mk00 mk01 mk10 mk11 ck00 ck01 ck10 ck11 ma0 ma1 ca0 ca1 y00 y01 y10 y11 "
              "m00 m01 m02 m03 m10 m11 m12 m13 c00 c01 c02 c03 c10 c11 c12 c13 g00 g01 g02 g03 g10 g11 g12 g13").split()


def send_masks(core, dests, topo):
    near = [d for d in dests if topo.die(d) == topo.die(core)]
    far = [d for d in dests if topo.die(d) != topo.die(core)]
    masks = {}
    for group, first in ((far, 0), (near, 1)):
        for k, d in enumerate(group):
            e = topo.engines(core, d)
            masks[d] = (1 << e[4 * k + first]) | (1 << e[4 * k + first + 2])
    return masks


def rank_program(g, core, T, topo):
    rank = T.rank_of(core)
    if rank is None:
        return
    S = T.sem
    v, a, t, sy = g.vector, g.scalar, g.tensor, g.sync
    COPY, IDENT = ActivationFunctionType.Copy, ActivationFunctionType.Identity
    A = AluOpType
    half, pos = rank // HALF, rank % HALF
    halves = (1 - half, half)

    def copy(q, out, win, sem):
        if q is v:
            v.tensor_copy(out, win).then_inc(S[sem], 1)
        else:
            a.activation(out, win, COPY).then_inc(S[sem], 1)

    for h in range(2):
        sy.dma_start(T.xb[:, 512 * h:512 * h + 512], T.x[:, 512 * h:512 * h + 512]).then_inc(S["lx%d" % h], 16)
    for k in range(8):
        a.dma_start(T.sl[16 * k:16 * k + 16, :], T.snd[:, :]).then_inc(S.lsnd, 16)
    for k in range(8):
        sy.dma_start(T.pl[16 * k:16 * k + 16, :], T.plc[:, :]).then_inc(S.lplc, 16)
    sy.dma_start(T.qb[:], T.qw[:, :]).then_inc(S.lqw, 16)
    sy.dma_start(T.kb[:], T.kc[:, :]).then_inc(S.lkc, 16)

    g.iota(T.dg[:], [[-1, 128]], 0, 1, allow_small_or_imprecise_dtypes=True).then_inc(S.dg, 1)
    v.memset(T.ez[:], 0.0).then_inc(S.ez0, 1)
    v.wait_ge(S.dg, 1)
    v.wait_ge(S.ez0, 1)
    v.tensor_scalar(T.ez[:, 3:515:4], T.dg[:], 0.0, None, A.is_equal).then_inc(S.ez, 1)
    g.iota(T.tab[:, 0:64], [[256, 2], [-16, 2], [16, 16]], 16, 0, allow_small_or_imprecise_dtypes=True).then_inc(S.tab, 1)
    g.iota(T.tab[:, 64:96], [[-16, 2], [0, 16]], 16, 0, allow_small_or_imprecise_dtypes=True).then_inc(S.tab, 1)
    g.iota(T.tab[:, 96:128], [[0, 2], [1, 16]], 0, 0, allow_small_or_imprecise_dtypes=True).then_inc(S.tab, 1)
    g.iota(T.far[:], [[0, 1]], FAR, 0, allow_small_or_imprecise_dtypes=True).then_inc(S.far, 1)
    g.iota(T.jc[:], [[16, 32]], XC, 0, allow_small_or_imprecise_dtypes=True).then_inc(S.jc, 1)
    g.iota(T.kneg[:], [[-16, 16]], -VI, -1).then_inc(S.kneg, 1)
    nv = 0
    for at, n, base in ((HC * halves[0], HC, 0), (HC * half, CAPP * pos, HC), (CAPP * rank, CAPP, ARR),
                        (CAPP * rank + CAPP, HC - CAPP * pos - CAPP, HC + CAPP * pos)):
        if n:
            g.iota(T.vals[:, at:at + n], [[1, n]], base, 0, allow_small_or_imprecise_dtypes=True).then_inc(S.vals, 1)
            nv += 1

    def quant_e(b):
        v.wait_ge(S.ez, 1)
        v.quantize_mx(T.eq[:, 128 * b:128 * b + 128], T.es[:, 128 * b:128 * b + 128], T.ez[:, 3 - b:3 - b + 512]).then_inc(S["eq%d" % b], 1)

    def quant_x(h):
        v.wait_ge(S["lx%d" % h], 16)
        v.quantize_mx(T.xq[:, HC * h:HC * h + HC], T.xs[:, HC * h:HC * h + HC],
                      T.xb[:, 512 * h:512 * h + 512]).then_inc(S["qx%d" % h], 1)

    def tables():
        v.wait_ge(S.tab, 3)
        v.transpose(T.tabt[:], T.tab[:]).then_inc(S.tabt, 1)

    def unpack(q, h, b):
        q.wait_ge(S["m%d%d" % (h, b)], 1)
        copy(q, T["xd%d" % b][:, HC * h:HC * h + HC], T[("pd%d", "py%d")[h] % b][:, 0:HC], "c%d%d" % (h, b))

    def offsets():
        v.wait_ge(S.lsnd, 128)
        v.tensor_copy(T.so[:], T.sl[:]).then_inc(S.conv, 1)

    def pick(q, ph, b):
        q.wait_ge(S.conv, 1)
        q.wait_ge(S["c0%d" % b], 1)
        q.wait_ge(S["c1%d" % b], 1)
        c = 2 * HALF * halves[ph]
        copy(q, T["hb%d" % ph][:, b:512:4], T["xd%d" % b][:, 0:XC].indirect(T.so[:, c:c + 2 * HALF]), "g%d%d" % (ph, b))

    def quant_h(ph):
        for b in range(4):
            v.wait_ge(S["g%d%d" % (ph, b)], 1)
        v.quantize_mx(T["hq%d" % ph][:], T["hs%d" % ph][:], T["hb%d" % ph][:]).then_inc(S["hq%d" % ph], 1)

    for h in range(2):
        t.wait_ge(S["qx%d" % h], 1)
        for b in range(4):
            t.wait_ge(S["eq%d" % b], 1)
            t.matmul_mx(T[("pd%d", "py%d")[h] % b][:, 0:HC], T.eq[:, 128 * b:128 * b + 128], T.es[:, 128 * b:128 * b + 128],
                        T.xq[:, HC * h:HC * h + HC], T.xs[:, HC * h:HC * h + HC], True, True).then_inc(S["m%d%d" % (h, b)], 1)
    for q, steps in ((v, VSTEPS), (a, ASTEPS)):
        for w in steps.split():
            n = [int(c) for c in w[1:]]
            if w[0] == "e":
                quant_e(*n)
            elif w[0] == "t":
                tables()
            elif w[0] == "x":
                quant_x(*n)
            elif w[0] == "c":
                unpack(q, *n)
            elif w[0] == "o":
                offsets()
            elif w[0] == "p":
                pick(q, *n)
            elif w[0] == "h":
                quant_h(*n)
            elif w[0] == "f":
                a.wait_ge(S.far, 1)
                a.wait_ge(S.ez, 1)
                a.activation(T.vl[:, 0:VI], T.ez[:], IDENT, bias=T.far[:, 0:1], scale=0.0).then_inc(S.vinit, 1)
            else:
                a.wait_ge(S.tabt, 1)
                a.wait_ge(S.jc, 1)
                a.activation(T.jt[:], T.jc[:], IDENT, bias=T.tabt[:, 96:97]).then_inc(S.jt, 1)

    masks = send_masks(core, [c for c in T.cores if c != core], topo)
    for planes, parts in CALLS:
        tr = []
        for ph in parts:
            g.wait_ge(S["hq%d" % ph], 1)
            for k in range(HALF):
                d = HALF * halves[ph] + k
                if d == rank:
                    continue
                dst = T.cores[d]
                rid, pid = topo.addr(dst)[:2]
                lo = CAPP * k
                at = HC * ph + CAPP * (pos - (1 if ph and rank > d else 0))
                if planes:
                    src, out = T["hs%d" % ph][:, lo:lo + CAPP], T.asc[:, at:at + CAPP]
                else:
                    src, out = T["hq%d" % ph][:, lo:lo + CAPP].bitcast(dt.uint8), T.aq[:, at:at + CAPP].bitcast(dt.uint8)
                tr.append(RemoteDMATransfer(dst_ids=[DstId(rid=rid, pnc=pid)], dma_engine_mask=masks[dst],
                                            remote_sem=S.arr, srcs=[src], dsts=[out]))
        g.remote_dma_fused(tr, local_sem=S.sent)

    v.wait_ge(S.lplc, 128)
    v.wait_ge(S.kneg, 1)
    v.tensor_tensor(T.nk[:], T.pl[:], T.kneg[:], A.mult).then_inc(S.ia, 1)
    v.wait_ge(S.lqw, 16)
    v.quantize_mx(T.wq[:], T.ws[:], T.qb[:]).then_inc(S.wq, 1)
    v.wait_ge(S.ia, 1)
    v.tensor_tensor(T.pm[:], T.nk[:], T.pl[:], A.max).then_inc(S.ib, 1)
    v.wait_ge(S.lkc, 16)
    v.quantize_mx(T.kq[:, 0:256], T.ks[:, 0:256], T.kb[:, 0:1024]).then_inc(S.kq0, 1)
    v.wait_ge(S.ib, 1)
    v.wait_ge(S.tabt, 1)
    v.tensor_scalar(T.po[:], T.pm[:], T.tabt[:, 64:65], None, A.add).then_inc(S.ic, 1)
    v.quantize_mx(T.kq[:, 256:512], T.ks[:, 256:512], T.kb[:, 1024:2048]).then_inc(S.kq1, 1)
    v.wait_ge(S.ic, 1)
    v.wait_ge(S.vals, nv)
    v.wait_ge(S.vinit, 1)
    v.tensor_copy(T.vl[:, 0:VW].indirect(T.po[:, 0:16]), T.vals[:, 0:XC]).then_inc(S.ie, 1)
    v.tensor_copy(T.eoff[:], T.tabt[:, 0:64:32]).then_inc(S.eoff, 1)
    v.wait_ge(S.ie, 1)
    v.transpose(T.tr[:], T.vl[:, 0:VI]).then_inc(S.it, 1)
    v.wait_ge(S.it, 1)
    v.wait_ge(S.eoff, 1)
    v.wait_ge(S.jt, 1)
    v.tensor_tensor(T.sf[:], T.tr[:, 0:VI].indirect(T.eoff[:, 0:2]), T.jt[:], A.min).then_inc(S.iu, 1)
    v.wait_ge(S.iu, 1)
    v.tensor_copy(T.inv[:], T.sf[:]).then_inc(S.inv, 1)

    def product(bank, o, q, s, n, sem):
        t.matmul_mx(T[bank][:, 0:n], T.wq[:, 128 * o:128 * o + 128], T.ws[:, 128 * o:128 * o + 128], q, s, True, True).then_inc(S[sem], 1)
    t.wait_ge(S.wq, 1)
    for h, bank in ((0, "py%d"), (1, "pd%d")):
        t.wait_ge(S["kq%d" % h], 1)
        for o in range(2):
            t.wait_ge(S["c%d%d" % (1 - h, o)], 1)
            product(bank % o, o, T.kq[:, 256 * h:256 * h + 256], T.ks[:, 256 * h:256 * h + 256], 256, "mk%d%d" % (h, o))
            a.wait_ge(S["mk%d%d" % (h, o)], 1)
            copy(a, T["w%d" % o][:, XC + 256 * h:XC + 256 * h + 256], T[bank % o][:, 0:256], "ck%d%d" % (h, o))
    for o in range(2):
        bank = "py%d" % (2 + o)
        t.wait_ge(S["c1%d" % (2 + o)], 1)
        product(bank, o, T.hq1[:], T.hs1[:], HC, "mo%d" % o)
        a.wait_ge(S["mo%d" % o], 1)
        copy(a, T["w%d" % o][:, ARR:XC], T[bank][:, CAPP * pos:CAPP * pos + CAPP], "co%d" % o)

    t.wait_ge(S.arr, 2 * 2 * (N - 1))
    for o in range(2):
        t.wait_ge(S["c0%d" % (2 + o)], 1)
        product("pd%d" % (2 + o), o, T.aq[:], T.asc[:], ARR, "ma%d" % o)

    for o, q in ((0, v), (1, a)):
        q.wait_ge(S["ma%d" % o], 1)
        copy(q, T["w%d" % o][:, 0:ARR], T["pd%d" % (2 + o)][:, 0:ARR], "ca%d" % o)
        for s in ("co%d", "ck0%d", "ck1%d", "ca%d"):
            q.wait_ge(S[s % o], 1)
        q.wait_ge(S.inv, 1)
        for i, (at, n) in enumerate(YP):
            copy(q, T["y%d" % o][:, at:at + n], T["w%d" % o][:, 0:TC + XC].indirect(T.inv[:, at // 16:(at + n) // 16]), "y%d%d" % (o, i))
    for i, (at, n) in enumerate(YP):
        for o in range(2):
            sy.wait_ge(S["y%d%d" % (o, i)], 1)
            sy.dma_start(T.y[:, TC * o + at:TC * o + at + n], T["y%d" % o][:, at:at + n]).then_inc(S.out, 16)
    sy.wait_ge(S.out, 16 * 2 * len(YP))
    g.wait_ge(S.sent, 2 * 2 * (N - 1))
